import numpy as np, ml_dtypes
CORES = [26,28,98,100,106,108,122,124]
N = 8
TK = 512
def setup_inputs(rng):
    return {"x": rng.standard_normal((N, 128, TK), dtype=np.float32).astype(ml_dtypes.bfloat16), "w1": (rng.standard_normal((N, 128, 128), dtype=np.float32) / 8).astype(ml_dtypes.bfloat16), "w2": (rng.standard_normal((N, 128, 128), dtype=np.float32) / 8).astype(ml_dtypes.bfloat16)}
def setup_inputs_big(rng):
    d = setup_inputs(rng)
    for k in ("x", "w1", "w2"): d[k] = (d[k].astype(np.float32) * 1024.0).astype(d[k].dtype)
    return d
def setup_inputs_small(rng):
    d = setup_inputs(rng)
    for k in ("x", "w1", "w2"): d[k] = (d[k].astype(np.float32) * (1 / 1024.0)).astype(d[k].dtype)
    return d
def setup_inputs_apart(rng):
    d = setup_inputs(rng)
    f = (10.0 ** rng.permutation(np.linspace(-1.5, 1.5, N))).astype(np.float32).reshape(N, 1, 1)
    for k in ("x", "w1", "w2"): d[k] = (d[k].astype(np.float32) * f).astype(d[k].dtype)
    return d
def reference(x, w1, w2):
    X, W1, W2 = x.astype(np.float64), w1.astype(np.float64), w2.astype(np.float64)
    y = np.zeros((N, 128, TK))
    for r in range(N):
        for j in range(N):
            y[r] += W2[j].T @ np.maximum(W1[j].T @ X[r], 0.0)
    return {"y": y.astype(ml_dtypes.bfloat16 if x.dtype != np.float64 else np.float64)}

@@ -1,0 +1,190 @@
+from concourse.bass import DstId, RemoteDMATransfer
+from concourse.mybir import dt, AluOpType
+
+N = 8
+TK = 512
+BW = 256
+C = 2
+CW = TK // C
+
+SCRATCH = {
+    "W": ("sbuf", [128, N * BW], "bfloat16"),
+    "X": ("sbuf", [128, TK], "bfloat16"),
+    "Z": ("sbuf", [128, CW], "float32"),
+    "H": ("sbuf", [128, 2 * TK], "bfloat16"),
+    "Y": ("sbuf", [128, TK], "bfloat16"),
+}
+for _i in range(2 * C):
+    SCRATCH["ph%d" % _i] = ("psum", [128, 512], "float32")
+for _i in range(C):
+    SCRATCH["py%d" % _i] = ("psum", [128, 512], "float32")
+
+SEMAPHORES = ["wl", "xl", "sent", "zs", "m1", "rl", "m2"] + ["arr%d" % j for j in range(N)] \
+    + ["yc%d" % c for c in range(C)] + ["st%d" % c for c in range(C)]
+
+
+def _count(m):
+    return bin(m).count("1")
+
+
+def _plan(cores, topo):
+    chips = []
+    for c in cores:
+        if topo.chip(c) not in chips:
+            chips.append(topo.chip(c))
+    on = {ch: [c for c in cores if topo.chip(c) == ch] for ch in chips}
+    every = range(topo.CHIPS * topo.CORES_PER_CHIP)
+    calls = {c: [] for c in cores}
+    arrive = {}
+    passes = {c: [] for c in cores}
+    used = set(cores)
+    relays = []
+
+    def far_mask(src):
+        other = [c for c in cores if topo.chip(c) != topo.chip(src)][0]
+        return topo.mask(src, other)
+
+    def mask_of(src, dst):
+        m = topo.mask(src, dst)
+        if topo.chip(src) == topo.chip(dst):
+            near = m & ~far_mask(src)
+            return near if near else m
+        return m
+
+    for j, o in enumerate(cores):
+        X = topo.chip(o)
+        p = chips.index(X)
+        direct, helped = [], []
+        for s in range(1, len(chips)):
+            Y = chips[(p + s) % len(chips)]
+            same = [t for t in on[Y] if topo.die(t) == topo.die(o)] or on[Y]
+            t = same[0]
+            if topo.may_write(o, t):
+                direct.append((t, [r for r in on[Y] if r != t]))
+            else:
+                free = [h for h in every if topo.chip(h) == X and h not in used
+                        and all(topo.may_write(h, r) for r in on[Y])]
+                free.sort(key=lambda h: (topo.die(h) != topo.die(o), h))
+                used.add(free[0])
+                helped.append((free[0], Y))
+        seq = []
+        if helped:
+            seq.append([h for h, _ in helped])
+        for t, rest in direct:
+            seq.append([t])
+        partners = [r for r in on[X] if r != o]
+        if partners:
+            seq.append(partners)
+        for idx, dsts in enumerate(seq):
+            calls[o].append((j, dsts, False))
+            for d in dsts:
+                arrive[(d, j)] = ((1, idx, j), _count(mask_of(o, d)))
+        for t, rest in direct:
+            if rest:
+                passes[t].append((arrive[(t, j)][0], j, rest))
+        for h, Y in helped:
+            relays.append((h, j, on[Y]))
+    for t in cores:
+        for n, (key, j, rest) in enumerate(sorted(passes[t])):
+            calls[t].append((j, rest, True))
+            for d in rest:
+                arrive[(d, j)] = ((2, n, j), _count(mask_of(t, d)))
+    for h, j, dsts in relays:
+        calls[h] = [(j, dsts, True)]
+        for d in dsts:
+            arrive[(d, j)] = ((3, 0, j), _count(mask_of(h, d)))
+    return calls, arrive, mask_of
+
+
+def rank_program(g, core, T, topo):
+    cores = list(T.cores)
+    calls, arrive, mask_of = _plan(cores, topo)
+    if core not in calls:
+        return
+    rank = T.rank_of(core)
+    sem = T.sem
+
+    def blk(j):
+        return T.W[:, j * BW:(j + 1) * BW]
+
+    if rank is not None:
+        g.sync.dma_start(T.W[:, rank * BW:rank * BW + 128], T.w1[:, :]).then_inc(sem.wl, 16)
+        g.scalar.dma_start(T.W[:, rank * BW + 128:(rank + 1) * BW], T.w2[:, :]).then_inc(sem.wl, 16)
+        g.sync.dma_start(T.X[:, 0:TK // 2], T.x[:, 0:TK // 2]).then_inc(sem.xl, 16)
+        g.scalar.dma_start(T.X[:, TK // 2:TK], T.x[:, TK // 2:TK]).then_inc(sem.xl, 16)
+        g.wait_ge(sem.wl, 32)
+
+    sent = 0
+    for j, dsts, waits in calls[core]:
+        if waits:
+            g.wait_ge(sem["arr%d" % j], arrive[(core, j)][1])
+        m = mask_of(core, dsts[0])
+        if len(dsts) == 1:
+            rid, pid, _ = topo.addr(dsts[0])
+            g.remote_dma(blk(j), blk(j), sem["arr%d" % j], sem.sent, pid, rid, m)
+        else:
+            ids = []
+            for d in dsts:
+                rid, pid, _ = topo.addr(d)
+                ids.append(DstId(rid=rid, pnc=pid))
+            g.remote_dma_fused([RemoteDMATransfer(dst_ids=ids, dma_engine_mask=m, remote_sem=sem["arr%d" % j],
+                                                  srcs=[blk(j)], dsts=[blk(j) for _ in dsts], alu_op=0)],
+                               local_sem=sem.sent)
+        sent += _count(m)
+    if sent:
+        g.wait_ge(sem.sent, sent)
+    if rank is None:
+        return
+
+    order = [rank] + sorted([j for j in range(N) if j != rank], key=lambda j: arrive[(core, j)][0])
+    te, ve = g.tensor, g.vector
+
+    def arrived(k):
+        j = order[k]
+        te.wait_ge(sem["arr%d" % j], arrive[(core, j)][1])
+
+    def mm1(k):
+        j = order[k]
+        for c in range(C):
+            te.matmul(T["ph%d" % ((k % 2) * C + c)][:, 0:CW], T.W[:, j * BW:j * BW + 128],
+                      T.X[:, c * CW:(c + 1) * CW], start=True, stop=True).then_inc(sem.m1, 1)
+
+    def mm2(k):
+        j = order[k]
+        for c in range(C):
+            te.wait_ge(sem.rl, k * C + c + 1)
+            a = (k % 2) * TK + c * CW
+            te.matmul(T["py%d" % c][:, 0:CW], T.W[:, j * BW + 128:(j + 1) * BW], T.H[:, a:a + CW],
+                      start=(k == 0), stop=(k == N - 1)).then_inc(sem.m2, 1)
+
+    te.wait_ge(sem.wl, 32)
+    te.wait_ge(sem.xl, 32)
+    mm1(0)
+    for k in range(1, N - 1):
+        arrived(k)
+        mm1(k)
+        mm2(k - 1)
+    mm2(N - 2)
+    arrived(N - 1)
+    mm1(N - 1)
+    mm2(N - 1)
+
+    ve.memset(T.Z[:, :], 0.0).then_inc(sem.zs, 1)
+    ve.wait_ge(sem.zs, 1)
+    for k in range(N):
+        for c in range(C):
+            ve.wait_ge(sem.m1, k * C + c + 1)
+            if k >= 2:
+                ve.wait_ge(sem.m2, (k - 2) * C + c + 1)
+            a = (k % 2) * TK + c * CW
+            ve.tensor_tensor(T.H[:, a:a + CW], T["ph%d" % ((k % 2) * C + c)][:, 0:CW], T.Z[:, :],
+                             AluOpType.max).then_inc(sem.rl, 1)
+    for c in range(C):
+        ve.wait_ge(sem.m2, (N - 1) * C + c + 1)
+        ve.tensor_copy(T.Y[:, c * CW:(c + 1) * CW], T["py%d" % c][:, 0:CW]).then_inc(sem["yc%d" % c], 1)
+
+    for c in range(C):
+        q = g.sync if c % 2 == 0 else g.scalar
+        q.wait_ge(sem["yc%d" % c], 1)
+        q.dma_start(T.y[:, c * CW:(c + 1) * CW], T.Y[:, c * CW:(c + 1) * CW]).then_inc(sem["st%d" % c], 16)
+        q.wait_ge(sem["st%d" % c], 16)

@@ -160,13 +160,10 @@ def rank_program(g, core, T, topo):
     te.wait_ge(sem.wl, 32)
     te.wait_ge(sem.xl, 32)
     mm1(0)
-    for k in range(1, N - 1):
+    for k in range(1, N):
         arrived(k)
         mm1(k)
         mm2(k - 1)
-    mm2(N - 2)
-    arrived(N - 1)
-    mm1(N - 1)
     mm2(N - 1)
 
     ve.memset(T.Z[:, :], 0.0).then_inc(sem.zs, 1)

from concourse.bass import DstId, RemoteDMATransfer
from concourse.mybir import dt, AluOpType

N = 8
TK = 512
BW = 256
C = 2
CW = TK // C

SCRATCH = {
    "W": ("sbuf", [128, N * BW], "bfloat16"),
    "X": ("sbuf", [128, TK], "bfloat16"),
    "Z": ("sbuf", [128, CW], "float32"),
    "H": ("sbuf", [128, 2 * TK], "bfloat16"),
    "Y": ("sbuf", [128, TK], "bfloat16"),
}
for _i in range(2 * C):
    SCRATCH["ph%d" % _i] = ("psum", [128, 512], "float32")
for _i in range(C):
    SCRATCH["py%d" % _i] = ("psum", [128, 512], "float32")

SEMAPHORES = ["wl", "xl", "sent", "zs", "m1", "rl", "m2"] + ["arr%d" % j for j in range(N)] \
    + ["yc%d" % c for c in range(C)] + ["st%d" % c for c in range(C)]


def _count(m):
    return bin(m).count("1")


def _plan(cores, topo):
    chips = []
    for c in cores:
        if topo.chip(c) not in chips:
            chips.append(topo.chip(c))
    on = {ch: [c for c in cores if topo.chip(c) == ch] for ch in chips}
    every = range(topo.CHIPS * topo.CORES_PER_CHIP)
    calls = {c: [] for c in cores}
    arrive = {}
    passes = {c: [] for c in cores}
    used = set(cores)
    relays = []

    def far_mask(src):
        other = [c for c in cores if topo.chip(c) != topo.chip(src)][0]
        return topo.mask(src, other)

    def mask_of(src, dst):
        m = topo.mask(src, dst)
        if topo.chip(src) == topo.chip(dst):
            near = m & ~far_mask(src)
            return near if near else m
        return m

    for j, o in enumerate(cores):
        X = topo.chip(o)
        p = chips.index(X)
        direct, helped = [], []
        for s in range(1, len(chips)):
            Y = chips[(p + s) % len(chips)]
            same = [t for t in on[Y] if topo.die(t) == topo.die(o)] or on[Y]
            t = same[0]
            if topo.may_write(o, t):
                direct.append((t, [r for r in on[Y] if r != t]))
            else:
                free = [h for h in every if topo.chip(h) == X and h not in used
                        and all(topo.may_write(h, r) for r in on[Y])]
                free.sort(key=lambda h: (topo.die(h) != topo.die(o), h))
                used.add(free[0])
                helped.append((free[0], Y))
        seq = []
        if helped:
            seq.append([h for h, _ in helped])
        for t, rest in direct:
            seq.append([t])
        partners = [r for r in on[X] if r != o]
        if partners:
            seq.append(partners)
        for idx, dsts in enumerate(seq):
            calls[o].append((j, dsts, False))
            for d in dsts:
                arrive[(d, j)] = ((1, idx, j), _count(mask_of(o, d)))
        for t, rest in direct:
            if rest:
                passes[t].append((arrive[(t, j)][0], j, rest))
        for h, Y in helped:
            relays.append((h, j, on[Y]))
    for t in cores:
        for n, (key, j, rest) in enumerate(sorted(passes[t])):
            calls[t].append((j, rest, True))
            for d in rest:
                arrive[(d, j)] = ((2, n, j), _count(mask_of(t, d)))
    for h, j, dsts in relays:
        calls[h] = [(j, dsts, True)]
        for d in dsts:
            arrive[(d, j)] = ((3, 0, j), _count(mask_of(h, d)))
    return calls, arrive, mask_of


def rank_program(g, core, T, topo):
    cores = list(T.cores)
    calls, arrive, mask_of = _plan(cores, topo)
    if core not in calls:
        return
    rank = T.rank_of(core)
    sem = T.sem

    def blk(j):
        return T.W[:, j * BW:(j + 1) * BW]

    if rank is not None:
        g.sync.dma_start(T.W[:, rank * BW:rank * BW + 128], T.w1[:, :]).then_inc(sem.wl, 16)
        g.scalar.dma_start(T.W[:, rank * BW + 128:(rank + 1) * BW], T.w2[:, :]).then_inc(sem.wl, 16)
        g.sync.dma_start(T.X[:, 0:TK // 2], T.x[:, 0:TK // 2]).then_inc(sem.xl, 16)
        g.scalar.dma_start(T.X[:, TK // 2:TK], T.x[:, TK // 2:TK]).then_inc(sem.xl, 16)
        g.wait_ge(sem.wl, 32)

    sent = 0
    for j, dsts, waits in calls[core]:
        if waits:
            g.wait_ge(sem["arr%d" % j], arrive[(core, j)][1])
        m = mask_of(core, dsts[0])
        if len(dsts) == 1:
            rid, pid, _ = topo.addr(dsts[0])
            g.remote_dma(blk(j), blk(j), sem["arr%d" % j], sem.sent, pid, rid, m)
        else:
            ids = []
            for d in dsts:
                rid, pid, _ = topo.addr(d)
                ids.append(DstId(rid=rid, pnc=pid))
            g.remote_dma_fused([RemoteDMATransfer(dst_ids=ids, dma_engine_mask=m, remote_sem=sem["arr%d" % j],
                                                  srcs=[blk(j)], dsts=[blk(j) for _ in dsts], alu_op=0)],
                               local_sem=sem.sent)
        sent += _count(m)
    if sent:
        g.wait_ge(sem.sent, sent)
    if rank is None:
        return

    order = [rank] + sorted([j for j in range(N) if j != rank], key=lambda j: arrive[(core, j)][0])
    te, ve = g.tensor, g.vector

    def arrived(k):
        j = order[k]
        te.wait_ge(sem["arr%d" % j], arrive[(core, j)][1])

    def mm1(k):
        j = order[k]
        for c in range(C):
            te.matmul(T["ph%d" % ((k % 2) * C + c)][:, 0:CW], T.W[:, j * BW:j * BW + 128],
                      T.X[:, c * CW:(c + 1) * CW], start=True, stop=True).then_inc(sem.m1, 1)

    def mm2(k):
        j = order[k]
        for c in range(C):
            te.wait_ge(sem.rl, k * C + c + 1)
            a = (k % 2) * TK + c * CW
            te.matmul(T["py%d" % c][:, 0:CW], T.W[:, j * BW + 128:(j + 1) * BW], T.H[:, a:a + CW],
                      start=(k == 0), stop=(k == N - 1)).then_inc(sem.m2, 1)

    te.wait_ge(sem.wl, 32)
    te.wait_ge(sem.xl, 32)
    mm1(0)
    for k in range(1, N):
        arrived(k)
        mm1(k)
        mm2(k - 1)
    mm2(N - 1)

    ve.memset(T.Z[:, :], 0.0).then_inc(sem.zs, 1)
    ve.wait_ge(sem.zs, 1)
    for k in range(N):
        for c in range(C):
            ve.wait_ge(sem.m1, k * C + c + 1)
            if k >= 2:
                ve.wait_ge(sem.m2, (k - 2) * C + c + 1)
            a = (k % 2) * TK + c * CW
            ve.tensor_tensor(T.H[:, a:a + CW], T["ph%d" % ((k % 2) * C + c)][:, 0:CW], T.Z[:, :],
                             AluOpType.max).then_inc(sem.rl, 1)
    for c in range(C):
        ve.wait_ge(sem.m2, (N - 1) * C + c + 1)
        ve.tensor_copy(T.Y[:, c * CW:(c + 1) * CW], T["py%d" % c][:, 0:CW]).then_inc(sem["yc%d" % c], 1)

    for c in range(C):
        q = g.sync if c % 2 == 0 else g.scalar
        q.wait_ge(sem["yc%d" % c], 1)
        q.dma_start(T.y[:, c * CW:(c + 1) * CW], T.Y[:, c * CW:(c + 1) * CW]).then_inc(sem["st%d" % c], 16)
        q.wait_ge(sem["st%d" % c], 16)
